import numpy as np
import ml_dtypes


def mxq(x, axis, fmt="e4m3"):
    dtype, down = {"e4m3": (ml_dtypes.float8_e4m3fn, 7), "e5m2": (ml_dtypes.float8_e5m2, 14)}[fmt]
    v = np.moveaxis(np.asarray(x, np.float32).astype(ml_dtypes.bfloat16).astype(np.float64), axis, -1)
    blocks = v.reshape(v.shape[:-1] + (-1, 32))
    amax = np.abs(blocks).max(-1, keepdims=True)
    byte = np.maximum(np.where(amax > 0, np.frexp(amax)[1] - 1 + 127, 0) - down, 1)
    scale = np.exp2(byte - 127.0)
    codes = (blocks / scale).astype(np.float32).astype(dtype).astype(np.float64)
    return np.moveaxis((codes * scale).reshape(v.shape), -1, axis)


WIDE = False


def mx_kscale(k):
    if not WIDE:
        return np.ones(k)
    levels = np.array([10, -10, 5, -5, 0])
    if k % 512:
        return np.exp2(np.random.permutation(np.resize(levels, k // 32))).repeat(32)
    a = np.empty((k // 512, 16))
    for p in range(k // 512):
        a[p, :8] = np.random.permutation(np.resize(levels, 8))
        for g in range(8):
            far = levels[np.abs(levels - a[p, g]) >= 10]
            a[p, g + 8] = far[np.random.randint(len(far))]
    return np.exp2(a.ravel()).repeat(32)


BF16 = ml_dtypes.bfloat16


def bf(x):
    return np.asarray(x, np.float32).astype(BF16)


def f64(x):
    return np.asarray(x).astype(np.float64)


E2M1 = np.array([0.0, 0.5, 1.0, 1.5, 2.0, 3.0, 4.0, 6.0, -0.0, -0.5, -1.0, -1.5, -2.0, -3.0, -4.0, -6.0])


def pack_weight(w, fmt):
    k, n = w.shape
    w = f64(bf(w)).reshape(k // 32, 32, n)
    amax = np.abs(w).max(1)
    if fmt == "e4m3":
        byte = np.frexp(amax)[1] - 1 + 127 - 7
    else:
        mant, ex = np.frexp(amax / 6.0)
        byte = np.where(mant > 0.5, ex, ex - 1) + 127
    byte = np.clip(np.where(amax > 0, byte, 1), 1, 254)
    scaled = (w * np.exp2(127.0 - byte)[:, None, :]).reshape(k, n).astype(np.float32)
    by_word = np.ascontiguousarray(scaled.reshape(k // 512, 128, 4, n).transpose(0, 1, 3, 2))
    if fmt == "e4m3":
        words = by_word.astype(ml_dtypes.float8_e4m3fn).view(np.uint8)
    else:
        c = by_word.astype(ml_dtypes.float4_e2m1fn).view(np.uint8) & 0xF
        words = c[..., 0::2] | (c[..., 1::2] << 4)
    return np.ascontiguousarray(words), np.ascontiguousarray(byte.astype(np.uint8).reshape(k // 512, 16, n))


def unpack_weight(words, scales, fmt):
    g, p, n, _ = words.shape
    if fmt == "e4m3":
        vals = np.ascontiguousarray(words).view(ml_dtypes.float8_e4m3fn).astype(np.float64)
    else:
        nib = np.empty((g, p, n, 4), np.uint8)
        nib[..., 0::2] = words & 0xF
        nib[..., 1::2] = words >> 4
        vals = E2M1[nib]
    vals = vals * np.repeat(np.exp2(scales.astype(np.float64) - 127.0), 8, axis=1)[..., None]
    return vals.transpose(0, 1, 3, 2).reshape(g * 512, n)
def pack4(w):
    words, scales = pack_weight(w, "e2m1")
    return words.reshape(words.shape[0], 128, -1), scales


def unpack4(words, scales):
    return unpack_weight(words.reshape(words.shape[0], 128, -1, 2), scales, "e2m1")


N, D, F, H = 1024, 1024, 1024, 2
HEAD_GAIN = np.array([2.0, 1.0])
P_HIT = 0.3


def softplus(v):
    return np.maximum(v, 0.0) + np.log(1.0 + np.exp(-np.abs(v)))


def draw0():
    r, t = mx_kscale(D), mx_kscale(F)
    x = bf(np.random.standard_normal((N, D)))
    xbar = bf(np.random.standard_normal((N, D)))
    u = bf(np.random.uniform(0.0, 1.0, (N, D)))
    s = bf((1.0 + 0.1 * np.random.standard_normal(D)) * r)
    we_words, we_scales = pack4(np.random.standard_normal((D, F)) / np.sqrt(D) / r[:, None])
    return {"x": x,
            "xbar": xbar,
            "u": u,
            "s": s,
            "we_words": we_words,
            "we_scales": we_scales,
            "g": bf((1.0 + 0.1 * np.random.standard_normal(F)) * t),
            "wh": bf(np.random.standard_normal((H, F, D)) * HEAD_GAIN[:, None, None] / np.sqrt(F) / t[None, :, None])}


def corrupt(x, xbar, u, s):
    hit = u < P_HIT
    m = np.where(hit, 1.0, 0.0)
    xt = s[None, :] * np.where(hit, xbar, x)
    return m, xt


def encode(xt, we, g):
    return g[None, :] * np.tanh(mxq(xt, 1, "e4m3") @ we)


def core(x, xbar, u, s, we_words, we_scales, g, wh):
    x, xbar, u, s, g, wh = f64(x), f64(xbar), f64(u), f64(s), f64(g), f64(wh)
    we = unpack4(we_words, we_scales)
    m, xt = corrupt(x, xbar, u, s)
    h = encode(xt, we, g)
    hq = mxq(h, 1, "e4m3")
    whq = mxq(wh, 1, "e4m3")
    a = hq @ whq[0]
    rec = hq @ whq[1]
    return softplus(a) - m * a + 2.0 * np.square(rec - x)


def e4m3fn_bytes(y):
    return np.clip(np.asarray(y, np.float64), -448.0, 448.0).astype(np.float32).astype(ml_dtypes.float8_e4m3fn).view(np.uint8)


def e4m3fn_values(b):
    return np.asarray(b, np.uint8).view(ml_dtypes.float8_e4m3fn).astype(np.float64)


def setup_inputs():
    d = draw0()
    x0 = np.asarray(d['wh']).astype(np.float64)
    s = (np.max(np.abs(x0), axis=(0, 2), keepdims=True) / 448.0).astype(np.float32)
    out = {}
    for k, v in d.items():
        if k == 'wh':
            out['wh_bytes'] = e4m3fn_bytes(x0 / s.astype(np.float64))
            out['wh_scale'] = s
        else:
            out[k] = v
    return out


def reference(x, xbar, u, s, we_words, we_scales, g, wh_bytes, wh_scale):
    return core(x, xbar, u, s, we_words, we_scales, g, e4m3fn_values(wh_bytes) * wh_scale.astype(np.float64))

@@ -1,0 +1,354 @@
+from contextlib import ExitStack
+
+import concourse.mybir as mybir
+from concourse.masks import make_identity
+
+F32 = mybir.dt.float32
+BF16 = mybir.dt.bfloat16
+U32 = mybir.dt.uint32
+I32 = mybir.dt.int32
+U8 = mybir.dt.uint8
+FP8 = mybir.dt.float8_e4m3fn
+FP8X4 = mybir.dt.float8_e4m3fn_x4
+FP4X4 = mybir.dt.float4_e2m1fn_x4
+ALU = mybir.AluOpType
+ACT = mybir.ActivationFunctionType
+
+P = 128
+N = 1024
+D = 1024
+F = 1024
+T = N // P
+P_HIT = 0.3
+LN_FLOOR = 1e-18
+SQRT2 = 2.0 ** 0.5
+
+G_TOTALS = (0, 1, 2, 3, 4, 5)
+
+STEP = [
+    ("x_turn", 2, -1),
+    ("w_quantize", 4, -1),
+    ("sigm", 17, -1),
+    ("load_tile", 0, -1),
+    ("h_quantize", 5, -1),
+    ("x_quantize", 3, -1),
+    ("w_widen", 1, 0),
+    ("sign_logit", 8, 0),
+    ("square", 35, -1),
+    ("recons", 29, 1),
+    ("recons", 27, 0),
+    ("encode", 3, 0),
+    ("squash", 3, 0),
+    ("h_gain", 4, 0),
+    ("mask", 0, -1),
+    ("load_we", 2, -1),
+    ("join", 1, -1),
+    ("sign_logit", 8, 1),
+    ("encode", 3, 1),
+    ("diff", 31, 1),
+    ("load_w_for", 0, -1),
+    ("w_interleave", 2, 0),
+    ("unmask", 0, -1),
+    ("logits", 7, 0),
+    ("logarithm", 32, -1),
+    ("x_drain", 2, -1),
+    ("squash", 3, 1),
+    ("pick_bar", 0, -1),
+    ("w_drain", 2, 0),
+    ("w_interleave", 2, 1),
+    ("w_widen", 1, 1),
+    ("h_gain", 4, 1),
+    ("h_turn", 3, 0),
+    ("logits", 7, 1),
+    ("smaller", 33, -1),
+    ("h_turn", 3, 1),
+    ("w_drain", 2, 1),
+    ("diff", 28, 0),
+    ("pick_x", 0, -1),
+    ("gain", 1, -1),
+    ("total", 46, 1),
+    ("total", 41, 0),
+]
+STEPS = 54
+
+FLOPS = 3 * 2 * N * D * F
+
+
+def tile_vimemaskandfeaturepretextloss_w4_kernel(
+    tc, x, xbar, u, s, we_words, we_scales, g, wh_bytes, wh_scale, out
+):
+    nc = tc.nc
+    with ExitStack() as ctx:
+        keep = ctx.enter_context(tc.tile_pool(name="keep", bufs=1))
+        pool = ctx.enter_context(tc.tile_pool(name="pool", bufs=2))
+        psum = ctx.enter_context(tc.psum_pool(name="psum", bufs=1))
+        ctx.enter_context(tc.manual_schedule())
+
+        x_sb, u_sb, xb_sb, m_sb, xt_sb, xg_sb, x8, xs8 = {}, {}, {}, {}, {}, {}, {}, {}
+        z_ps, th_sb, ht_ps, hg_sb, h8, hs8 = {}, {}, {}, {}, {}, {}
+        wb_sb, wide_sb, w_ps, wi_sb = {}, {}, {}, {}
+        a_ps, r_ps, y_sb, l_sb, d_sb = {}, {}, {}, {}, {}
+
+        def rows(i):
+            return slice(i * P, (i + 1) * P)
+
+        def load_tile(i):
+            u_sb[i] = pool.tile([P, D], BF16, tag="u", name="u_t", bufs=4)
+            nc.sync.dma_start(out=u_sb[i][:], in_=u[rows(i), :])
+            xb_sb[i] = pool.tile([P, D], BF16, tag="xb", name="xb_t", bufs=4)
+            nc.sync.dma_start(out=xb_sb[i][:], in_=xbar[rows(i), :])
+            x_sb[i] = keep.tile([P, D], BF16, tag="x%d" % i, name="x_t")
+            nc.sync.dma_start(out=x_sb[i][:], in_=x[rows(i), :])
+
+        def load_w(j, gg):
+            wb_sb[j, gg] = pool.tile([P, 4, D], U8, tag="wb", name="wb_t", bufs=2, align_bytes=64)
+            nc.sync.dma_start(
+                out=wb_sb[j, gg][:],
+                in_=wh_bytes[j].rearrange("(g p t) n -> g p t n", p=P, t=4)[gg],
+            )
+
+        s_row = keep.tile([P, D], BF16, tag="s_row", name="s_row")
+        nc.vector.memset(s_row[:], 0.0)
+        ones = keep.tile([P, P], BF16, tag="ones", name="ones")
+        nc.vector.memset(ones[:], 1.0)
+        wes = keep.tile([P, 2, F], U8, tag="wes", name="wes", align_bytes=64)
+        nc.vector.memset(wes[:].rearrange("p g n -> p (g n)").bitcast(U32), 0)
+        dummy = keep.tile([P, 1], F32, tag="dummy", name="dummy")
+        nc.scalar.activation(out=dummy[:], in_=ones[:, 0:1], func=ACT.Sigmoid)
+
+        wsc = keep.tile([P, 2, 4], F32, tag="wsc", name="wsc")
+        gcol = keep.tile([P, 2, 4], BF16, tag="gcol", name="gcol")
+        nc.scalar.dma_start(out=s_row[0:1, :], in_=s.rearrange("(o d) -> o d", o=1))
+        nc.scalar.dma_start(out=wsc[:], in_=wh_scale.rearrange("o (g p t) e -> p g (t o e)", p=P, t=4))
+        nc.scalar.dma_start(out=gcol[:], in_=g.rearrange("(c p t) -> p c t", p=P, t=4))
+
+        we = keep.tile([P, 2, 2 * F], U8, tag="we", name="we", align_bytes=64)
+
+        def load_we(i):
+            nc.sync.dma_start(out=we[:], in_=we_words.rearrange("g p b -> p g b"))
+            for q in range(4):
+                nc.sync.dma_start(
+                    out=wes[32 * q : 32 * q + 4, :, :].bitcast(I32),
+                    in_=we_scales[:, 4 * q : 4 * q + 4, :].bitcast(I32).rearrange("g q n -> q g n"),
+                )
+
+        def load_w_for(k):
+            if k in (0, 1, 4, 5):
+                load_w(k // 4, k % 2)
+
+        ident = keep.tile([P, P], F32, tag="ident", name="ident")
+        make_identity(nc, ident[:])
+        ident_b = keep.tile([P, P], BF16, tag="ident_b", name="ident_b")
+        nc.vector.tensor_copy(out=ident_b[:], in_=ident[:])
+
+        s_bc = keep.tile([P, D], BF16, tag="s_bc", name="s_bc")
+        for c in range(2):
+            s_ps = psum.tile([P, 512], F32, tag="z", name="s_ps", bufs=2)
+            nc.tensor.matmul(
+                out=s_ps[:], lhsT=ones[:], rhs=s_row[:, 512 * c : 512 * (c + 1)], start=True, stop=True
+            )
+            nc.scalar.copy(out=s_bc[:, 512 * c : 512 * (c + 1)], in_=s_ps[:])
+
+        w8 = {}
+        ws8 = {}
+        for j in range(2):
+            w8[j] = keep.tile([P, 2, D], U32, tag="w8_%d" % j, name="w8_t", align_bytes=64)
+            ws8[j] = keep.tile([P, 2, D], U8, tag="ws8_%d" % j, name="ws8_t", align_bytes=64)
+
+        def w_key(k):
+            return k // 4, k % 2, (k // 2) % 2
+
+        def w_widen(k, th):
+            j, gg, nh = w_key(k)
+            if th == 0:
+                wide_sb[k] = pool.tile([P, 4, 512], BF16, tag="wide", name="wide_t", bufs=2)
+            for t in (2 * th, 2 * th + 1):
+                nc.scalar.activation(
+                    out=wide_sb[k][:, t, :],
+                    in_=wb_sb[j, gg][:, t, 512 * nh : 512 * (nh + 1)].bitcast(FP8),
+                    func=ACT.Copy,
+                    scale=wsc[:, gg, t : t + 1],
+                )
+
+        def w_interleave(k, b):
+            w_ps[k, b] = psum.tile([P, 1024], BF16, tag="p", name="w_ps_t", bufs=4)
+            for q in range(2):
+                c0 = (2 * b + q) * P
+                nc.tensor.matmul(
+                    out=w_ps[k, b][:, 512 * q : 512 * (q + 1)].rearrange("p (n t) -> p n t", t=4),
+                    lhsT=ident_b[:],
+                    rhs=wide_sb[k][:, :, c0 : c0 + P].rearrange("p t n -> p n t"),
+                    start=True,
+                    stop=True,
+                )
+
+        def w_drain(k, b):
+            if b == 0:
+                wi_sb[k] = pool.tile([P, 2048], BF16, tag="wi", name="wi_t", bufs=2, align_bytes=64)
+            nc.scalar.copy(out=wi_sb[k][:, 1024 * b : 1024 * (b + 1)], in_=w_ps[k, b][:])
+
+        def w_quantize(k):
+            j, gg, nh = w_key(k)
+            cols = slice(512 * nh, 512 * (nh + 1))
+            nc.vector.quantize_mx(
+                out=w8[j][:, gg, cols].bitcast(FP8X4), scales=ws8[j][:, gg, cols], in_=wi_sb[k][:]
+            )
+
+        def mask(i):
+            m_sb[i] = keep.tile([P, D], BF16, tag="m%d" % i, name="m_t")
+            nc.vector.tensor_scalar(out=m_sb[i][:], in0=u_sb[i][:], scalar1=P_HIT, scalar2=None, op0=ALU.is_lt)
+
+        def unmask(i):
+            nc.vector.tensor_scalar(out=u_sb[i][:], in0=u_sb[i][:], scalar1=P_HIT, scalar2=None, op0=ALU.is_ge)
+
+        def pick_bar(i):
+            nc.vector.tensor_tensor(out=xb_sb[i][:], in0=m_sb[i][:], in1=xb_sb[i][:], op=ALU.mult)
+
+        def pick_x(i):
+            nc.vector.tensor_tensor(out=u_sb[i][:], in0=u_sb[i][:], in1=x_sb[i][:], op=ALU.mult)
+
+        def join(i):
+            nc.vector.tensor_tensor(out=xb_sb[i][:], in0=xb_sb[i][:], in1=u_sb[i][:], op=ALU.add)
+
+        def gain(i):
+            xt_sb[i] = pool.tile([P, D], BF16, tag="xt", name="xt_t", bufs=2)
+            nc.vector.tensor_tensor(out=xt_sb[i][:], in0=xb_sb[i][:], in1=s_bc[:], op=ALU.mult)
+
+        def x_turn(i):
+            x_ps = psum.tile([P, 4, P], F32, tag="p", name="x_ps_t", bufs=4)
+            words = xt_sb[i][:].bitcast(F32)
+            for gg in range(2):
+                for v in range(2):
+                    nc.tensor.transpose(
+                        x_ps[:, 2 * gg + v, :], words[:, 256 * gg + v : 256 * (gg + 1) : 2], ident[:]
+                    )
+            z_ps["x", i] = x_ps
+
+        def x_drain(i):
+            xg_sb[i] = pool.tile([P, D], BF16, tag="xg", name="xg_t", bufs=2, align_bytes=64)
+            nc.scalar.copy(
+                out=xg_sb[i][:].bitcast(F32).rearrange("p (g r v) -> p g r v", g=2, v=2),
+                in_=z_ps["x", i][:].rearrange("p (g v) r -> p g r v", g=2),
+            )
+
+        def x_quantize(i):
+            x8[i] = pool.tile([P, 256], U32, tag="x8", name="x8_t", bufs=2, align_bytes=64)
+            xs8[i] = pool.tile([P, 256], U8, tag="xs8", name="xs8_t", bufs=2, align_bytes=64)
+            nc.vector.quantize_mx(out=x8[i][:].bitcast(FP8X4), scales=xs8[i][:], in_=xg_sb[i][:])
+
+        def encode(i, c):
+            z_ps[i, c] = psum.tile([P, 512], F32, tag="z", name="z_ps_t", bufs=2)
+            for gg in range(2):
+                nc.tensor.matmul_mx(
+                    out=z_ps[i, c][:],
+                    lhsT=x8[i][:, P * gg : P * (gg + 1)].bitcast(FP8X4),
+                    lhsT_scale=xs8[i][:, P * gg : P * (gg + 1)],
+                    rhs=we[:, gg, 1024 * c : 1024 * (c + 1)].bitcast(FP4X4),
+                    rhs_scale=wes[:, gg, 512 * c : 512 * (c + 1)],
+                    start=(gg == 0),
+                    stop=(gg == 1),
+                )
+
+        def squash(i, c):
+            th_sb[i, c] = pool.tile([P, 4, P], F32, tag="th", name="th_t", bufs=3)
+            nc.scalar.activation(
+                out=th_sb[i, c][:], in_=z_ps[i, c][:].rearrange("p (m t) -> p t m", t=4), func=ACT.Tanh
+            )
+
+        def h_turn(i, c):
+            ht_ps[i, c] = psum.tile([P, 4, P], F32, tag="h", name="ht_ps_t", bufs=2)
+            for t in range(4):
+                nc.tensor.transpose(ht_ps[i, c][:, t, :], th_sb[i, c][:, t, :], ident[:])
+
+        def h_gain(i, c):
+            if c == 0:
+                hg_sb[i] = pool.tile([P, F], BF16, tag="hg", name="hg_t", bufs=2, align_bytes=64)
+            nc.vector.tensor_tensor(
+                out=hg_sb[i][:, 512 * c : 512 * (c + 1)].rearrange("p (r t) -> p r t", t=4),
+                in0=ht_ps[i, c][:].rearrange("p t r -> p r t"),
+                in1=gcol[:, c, :].unsqueeze(1).to_broadcast([P, P, 4]),
+                op=ALU.mult,
+            )
+
+        def h_quantize(i):
+            h8[i] = keep.tile([P, 256], U32, tag="h8_%d" % i, name="h8_t", align_bytes=64)
+            hs8[i] = keep.tile([P, 256], U8, tag="hs8_%d" % i, name="hs8_t", align_bytes=64)
+            nc.vector.quantize_mx(out=h8[i][:].bitcast(FP8X4), scales=hs8[i][:], in_=hg_sb[i][:])
+
+        def head(i, j, nh, tag):
+            bank = psum.tile([P, 512], F32, tag=tag, name="head_ps_t", bufs=4 if tag == "p" else 2)
+            cols = slice(512 * nh, 512 * (nh + 1))
+            for gg in range(2):
+                nc.tensor.matmul_mx(
+                    out=bank[:],
+                    lhsT=h8[i][:, P * gg : P * (gg + 1)].bitcast(FP8X4),
+                    lhsT_scale=hs8[i][:, P * gg : P * (gg + 1)],
+                    rhs=w8[j][:, gg, cols].bitcast(FP8X4),
+                    rhs_scale=ws8[j][:, gg, cols],
+                    start=(gg == 0),
+                    stop=(gg == 1),
+                )
+            return bank
+
+        def logits(i, nh):
+            a_ps[i, nh] = head(i, 0, nh, "p")
+
+        def recons(i, nh):
+            r_ps[i, nh] = head(i, 1, nh, "zp"[nh])
+
+        def sign_logit(i, nh):
+            if nh == 0:
+                y_sb[i] = keep.tile([P, D], F32, tag="y%d" % i, name="y_t")
+            cols = slice(512 * nh, 512 * (nh + 1))
+            nc.vector.scalar_tensor_tensor(
+                out=y_sb[i][:, cols], in0=m_sb[i][:, cols], scalar=0.5, in1=a_ps[i, nh][:],
+                op0=ALU.subtract, op1=ALU.mult,
+            )
+
+        def sigm(i):
+            l_sb[i] = keep.tile([P, D], F32, tag="l%d" % i, name="l_t")
+            nc.scalar.activation(out=l_sb[i][:], in_=y_sb[i][:], func=ACT.Sigmoid, scale=2.0)
+
+        def diff(i, nh):
+            if nh == 0:
+                d_sb[i] = keep.tile([P, D], F32, tag="d%d" % i, name="d_t")
+            cols = slice(512 * nh, 512 * (nh + 1))
+            nc.vector.tensor_tensor(
+                out=d_sb[i][:, cols], in0=r_ps[i, nh][:], in1=x_sb[i][:, cols], op=ALU.subtract
+            )
+
+        def square(i):
+            nc.scalar.activation(out=d_sb[i][:], in_=d_sb[i][:], func=ACT.Square, scale=SQRT2)
+
+        def logarithm(i):
+            nc.scalar.activation(out=l_sb[i][:], in_=l_sb[i][:], func=ACT.Ln, bias=LN_FLOOR)
+
+        def smaller(i):
+            nc.vector.scalar_tensor_tensor(
+                out=y_sb[i][:], in0=y_sb[i][:], scalar=2.0, in1=l_sb[i][:], op0=ALU.mult, op1=ALU.min
+            )
+
+        def total(i, half):
+            cols = slice(512 * half, 512 * (half + 1))
+            engine = nc.gpsimd if half == 0 and i in G_TOTALS else nc.vector
+            engine.tensor_tensor(
+                out=d_sb[i][:, cols], in0=d_sb[i][:, cols], in1=y_sb[i][:, cols], op=ALU.subtract
+            )
+            nc.sync.dma_start(out=out[rows(i), cols], in_=d_sb[i][:, cols])
+
+        calls = dict(
+            load_tile=load_tile, load_we=load_we, load_w_for=load_w_for, mask=mask, unmask=unmask,
+            pick_bar=pick_bar, pick_x=pick_x, join=join, gain=gain, x_turn=x_turn, x_drain=x_drain,
+            x_quantize=x_quantize, encode=encode, squash=squash, h_turn=h_turn, h_gain=h_gain,
+            h_quantize=h_quantize, w_widen=w_widen, w_interleave=w_interleave, w_drain=w_drain,
+            w_quantize=w_quantize, logits=logits, sign_logit=sign_logit, sigm=sigm, recons=recons,
+            diff=diff, square=square, logarithm=logarithm, smaller=smaller, total=total,
+        )
+        for step in range(STEPS):
+            for what, lag, half in STEP:
+                i = step - lag
+                if 0 <= i < (1 if what == "load_we" else T):
+                    if half < 0:
+                        calls[what](i)
+                    else:
+                        calls[what](i, half)

@@ -23,53 +23,51 @@ P_HIT = 0.3
 LN_FLOOR = 1e-18
 SQRT2 = 2.0 ** 0.5
 
-G_TOTALS = (0, 1, 2, 3, 4, 5)
-
 STEP = [
+    ("sign_logit", 7, 0),
+    ("x_quantize", 3, -1),
     ("x_turn", 2, -1),
-    ("w_quantize", 4, -1),
-    ("sigm", 17, -1),
+    ("encode", 3, 0),
+    ("logits", 6, 0),
+    ("squash", 3, 0),
+    ("encode", 3, 1),
+    ("w_interleave", 2, 0),
+    ("join", 1, -1),
     ("load_tile", 0, -1),
     ("h_quantize", 5, -1),
-    ("x_quantize", 3, -1),
-    ("w_widen", 1, 0),
-    ("sign_logit", 8, 0),
-    ("square", 35, -1),
-    ("recons", 29, 1),
-    ("recons", 27, 0),
-    ("encode", 3, 0),
-    ("squash", 3, 0),
-    ("h_gain", 4, 0),
-    ("mask", 0, -1),
-    ("load_we", 2, -1),
-    ("join", 1, -1),
-    ("sign_logit", 8, 1),
-    ("encode", 3, 1),
-    ("diff", 31, 1),
-    ("load_w_for", 0, -1),
-    ("w_interleave", 2, 0),
-    ("unmask", 0, -1),
-    ("logits", 7, 0),
-    ("logarithm", 32, -1),
-    ("x_drain", 2, -1),
-    ("squash", 3, 1),
-    ("pick_bar", 0, -1),
-    ("w_drain", 2, 0),
     ("w_interleave", 2, 1),
-    ("w_widen", 1, 1),
-    ("h_gain", 4, 1),
+    ("h_gain", 4, 0),
+    ("total", 68, -1),
+    ("mask", 0, -1),
+    ("recons", 33, 0),
+    ("load_w_for", 1, -1),
+    ("sign_logit", 7, 1),
+    ("unmask", 0, -1),
+    ("gain", 2, -1),
+    ("squash", 3, 1),
+    ("w_widen", 1, 0),
     ("h_turn", 3, 0),
-    ("logits", 7, 1),
-    ("smaller", 33, -1),
-    ("h_turn", 3, 1),
-    ("w_drain", 2, 1),
-    ("diff", 28, 0),
+    ("pick_bar", 0, -1),
+    ("diff", 34, 0),
+    ("logarithm", 29, -1),
+    ("smaller", 40, -1),
+    ("diff", 35, 1),
+    ("h_gain", 4, 1),
+    ("w_interleave", 2, 2),
     ("pick_x", 0, -1),
-    ("gain", 1, -1),
-    ("total", 46, 1),
-    ("total", 41, 0),
+    ("square", 50, -1),
+    ("recons", 34, 1),
+    ("load_we", 2, -1),
+    ("w_quantize", 3, -1),
+    ("logits", 6, 1),
+    ("w_interleave", 2, 3),
+    ("w_drain", 2, 0),
+    ("w_widen", 1, 1),
+    ("w_drain", 2, 1),
+    ("h_turn", 3, 1),
+    ("sigm", 13, -1),
 ]
-STEPS = 54
+STEPS = 76
 
 FLOPS = 3 * 2 * N * D * F
 
@@ -84,7 +82,7 @@ def tile_vimemaskandfeaturepretextloss_w4_kernel(
         psum = ctx.enter_context(tc.psum_pool(name="psum", bufs=1))
         ctx.enter_context(tc.manual_schedule())
 
-        x_sb, u_sb, xb_sb, m_sb, xt_sb, xg_sb, x8, xs8 = {}, {}, {}, {}, {}, {}, {}, {}
+        x_sb, u_sb, xb_sb, m_sb, x_ps, xg_sb, x8, xs8 = {}, {}, {}, {}, {}, {}, {}, {}
         z_ps, th_sb, ht_ps, hg_sb, h8, hs8 = {}, {}, {}, {}, {}, {}
         wb_sb, wide_sb, w_ps, wi_sb = {}, {}, {}, {}
         a_ps, r_ps, y_sb, l_sb, d_sb = {}, {}, {}, {}, {}
@@ -107,18 +105,17 @@ def tile_vimemaskandfeaturepretextloss_w4_kernel(
                 in_=wh_bytes[j].rearrange("(g p t) n -> g p t n", p=P, t=4)[gg],
             )
 
-        s_row = keep.tile([P, D], BF16, tag="s_row", name="s_row")
-        nc.vector.memset(s_row[:], 0.0)
-        ones = keep.tile([P, P], BF16, tag="ones", name="ones")
-        nc.vector.memset(ones[:], 1.0)
+        one = keep.tile([P, 1], BF16, tag="one", name="one")
+        nc.vector.memset(one[:], 1.0)
         wes = keep.tile([P, 2, F], U8, tag="wes", name="wes", align_bytes=64)
         nc.vector.memset(wes[:].rearrange("p g n -> p (g n)").bitcast(U32), 0)
         dummy = keep.tile([P, 1], F32, tag="dummy", name="dummy")
-        nc.scalar.activation(out=dummy[:], in_=ones[:, 0:1], func=ACT.Sigmoid)
+        nc.scalar.activation(out=dummy[:], in_=one[:], func=ACT.Sigmoid)
 
         wsc = keep.tile([P, 2, 4], F32, tag="wsc", name="wsc")
         gcol = keep.tile([P, 2, 4], BF16, tag="gcol", name="gcol")
-        nc.scalar.dma_start(out=s_row[0:1, :], in_=s.rearrange("(o d) -> o d", o=1))
+        scol = keep.tile([P, 2, 4], BF16, tag="scol", name="scol")
+        nc.scalar.dma_start(out=scol[:], in_=s.rearrange("(g p t) -> p g t", p=P, t=4))
         nc.scalar.dma_start(out=wsc[:], in_=wh_scale.rearrange("o (g p t) e -> p g (t o e)", p=P, t=4))
         nc.scalar.dma_start(out=gcol[:], in_=g.rearrange("(c p t) -> p c t", p=P, t=4))
 
@@ -141,14 +138,6 @@ def tile_vimemaskandfeaturepretextloss_w4_kernel(
         ident_b = keep.tile([P, P], BF16, tag="ident_b", name="ident_b")
         nc.vector.tensor_copy(out=ident_b[:], in_=ident[:])
 
-        s_bc = keep.tile([P, D], BF16, tag="s_bc", name="s_bc")
-        for c in range(2):
-            s_ps = psum.tile([P, 512], F32, tag="z", name="s_ps", bufs=2)
-            nc.tensor.matmul(
-                out=s_ps[:], lhsT=ones[:], rhs=s_row[:, 512 * c : 512 * (c + 1)], start=True, stop=True
-            )
-            nc.scalar.copy(out=s_bc[:, 512 * c : 512 * (c + 1)], in_=s_ps[:])
-
         w8 = {}
         ws8 = {}
         for j in range(2):
@@ -161,7 +150,7 @@ def tile_vimemaskandfeaturepretextloss_w4_kernel(
         def w_widen(k, th):
             j, gg, nh = w_key(k)
             if th == 0:
-                wide_sb[k] = pool.tile([P, 4, 512], BF16, tag="wide", name="wide_t", bufs=2)
+                wide_sb[k] = pool.tile([P, 4, 512], BF16, tag="wide", name="wide_t", bufs=3)
             for t in (2 * th, 2 * th + 1):
                 nc.scalar.activation(
                     out=wide_sb[k][:, t, :],
@@ -170,17 +159,17 @@ def tile_vimemaskandfeaturepretextloss_w4_kernel(
                     scale=wsc[:, gg, t : t + 1],
                 )
 
-        def w_interleave(k, b):
-            w_ps[k, b] = psum.tile([P, 1024], BF16, tag="p", name="w_ps_t", bufs=4)
-            for q in range(2):
-                c0 = (2 * b + q) * P
-                nc.tensor.matmul(
-                    out=w_ps[k, b][:, 512 * q : 512 * (q + 1)].rearrange("p (n t) -> p n t", t=4),
-                    lhsT=ident_b[:],
-                    rhs=wide_sb[k][:, :, c0 : c0 + P].rearrange("p t n -> p n t"),
-                    start=True,
-                    stop=True,
-                )
+        def w_interleave(k, part):
+            b, q = part // 2, part % 2
+            if q == 0:
+                w_ps[k, b] = psum.tile([P, 1024], BF16, tag="p", name="w_ps_t", bufs=4)
+            nc.tensor.matmul(
+                out=w_ps[k, b][:, 512 * q : 512 * (q + 1)].rearrange("p (n t) -> p n t", t=4),
+                lhsT=ident_b[:],
+                rhs=wide_sb[k][:, :, P * part : P * (part + 1)].rearrange("p t n -> p n t"),
+                start=True,
+                stop=True,
+            )
 
         def w_drain(k, b):
             if b == 0:
@@ -210,26 +199,27 @@ def tile_vimemaskandfeaturepretextloss_w4_kernel(
         def join(i):
             nc.vector.tensor_tensor(out=xb_sb[i][:], in0=xb_sb[i][:], in1=u_sb[i][:], op=ALU.add)
 
-        def gain(i):
-            xt_sb[i] = pool.tile([P, D], BF16, tag="xt", name="xt_t", bufs=2)
-            nc.vector.tensor_tensor(out=xt_sb[i][:], in0=xb_sb[i][:], in1=s_bc[:], op=ALU.mult)
-
         def x_turn(i):
-            x_ps = psum.tile([P, 4, P], F32, tag="p", name="x_ps_t", bufs=4)
-            words = xt_sb[i][:].bitcast(F32)
+            x_ps[i] = psum.tile([P, 4, P], F32, tag="p", name="x_ps_t", bufs=4)
+            words = xb_sb[i][:].bitcast(F32)
             for gg in range(2):
                 for v in range(2):
                     nc.tensor.transpose(
-                        x_ps[:, 2 * gg + v, :], words[:, 256 * gg + v : 256 * (gg + 1) : 2], ident[:]
+                        x_ps[i][:, 2 * gg + v, :], words[:, 256 * gg + v : 256 * (gg + 1) : 2], ident[:]
                     )
-            z_ps["x", i] = x_ps
 
-        def x_drain(i):
+        def gain(i):
             xg_sb[i] = pool.tile([P, D], BF16, tag="xg", name="xg_t", bufs=2, align_bytes=64)
-            nc.scalar.copy(
-                out=xg_sb[i][:].bitcast(F32).rearrange("p (g r v) -> p g r v", g=2, v=2),
-                in_=z_ps["x", i][:].rearrange("p (g v) r -> p g r v", g=2),
-            )
+            for gg in range(2):
+                nc.vector.tensor_tensor(
+                    out=xg_sb[i][:, 512 * gg : 512 * (gg + 1)].rearrange("p (r v e) -> p r v e", v=2, e=2),
+                    in0=x_ps[i][:, 2 * gg : 2 * gg + 2, :]
+                    .rearrange("p v r -> p (v r)")
+                    .bitcast(BF16)
+                    .rearrange("p (v r e) -> p r v e", v=2, e=2),
+                    in1=scol[:, gg, :].rearrange("p (v e) -> p v e", e=2).unsqueeze(1).to_broadcast([P, P, 2, 2]),
+                    op=ALU.mult,
+                )
 
         def x_quantize(i):
             x8[i] = pool.tile([P, 256], U32, tag="x8", name="x8_t", bufs=2, align_bytes=64)
@@ -328,17 +318,18 @@ def tile_vimemaskandfeaturepretextloss_w4_kernel(
                 out=y_sb[i][:], in0=y_sb[i][:], scalar=2.0, in1=l_sb[i][:], op0=ALU.mult, op1=ALU.min
             )
 
-        def total(i, half):
-            cols = slice(512 * half, 512 * (half + 1))
-            engine = nc.gpsimd if half == 0 and i in G_TOTALS else nc.vector
-            engine.tensor_tensor(
-                out=d_sb[i][:, cols], in0=d_sb[i][:, cols], in1=y_sb[i][:, cols], op=ALU.subtract
-            )
-            nc.sync.dma_start(out=out[rows(i), cols], in_=d_sb[i][:, cols])
+        def total(i):
+            parts = 2 if i == T - 1 else 1
+            for part in range(parts):
+                cols = slice(part * D // parts, (part + 1) * D // parts)
+                nc.vector.tensor_tensor(
+                    out=d_sb[i][:, cols], in0=d_sb[i][:, cols], in1=y_sb[i][:, cols], op=ALU.subtract
+                )
+                nc.sync.dma_start(out=out[rows(i), cols], in_=d_sb[i][:, cols])
 
         calls = dict(
             load_tile=load_tile, load_we=load_we, load_w_for=load_w_for, mask=mask, unmask=unmask,
-            pick_bar=pick_bar, pick_x=pick_x, join=join, gain=gain, x_turn=x_turn, x_drain=x_drain,
+            pick_bar=pick_bar, pick_x=pick_x, join=join, gain=gain, x_turn=x_turn,
             x_quantize=x_quantize, encode=encode, squash=squash, h_turn=h_turn, h_gain=h_gain,
             h_quantize=h_quantize, w_widen=w_widen, w_interleave=w_interleave, w_drain=w_drain,
             w_quantize=w_quantize, logits=logits, sign_logit=sign_logit, sigm=sigm, recons=recons,

from contextlib import ExitStack

import concourse.mybir as mybir
from concourse.masks import make_identity

F32 = mybir.dt.float32
BF16 = mybir.dt.bfloat16
U32 = mybir.dt.uint32
I32 = mybir.dt.int32
U8 = mybir.dt.uint8
FP8 = mybir.dt.float8_e4m3fn
FP8X4 = mybir.dt.float8_e4m3fn_x4
FP4X4 = mybir.dt.float4_e2m1fn_x4
ALU = mybir.AluOpType
ACT = mybir.ActivationFunctionType

P = 128
N = 1024
D = 1024
F = 1024
T = N // P
P_HIT = 0.3
LN_FLOOR = 1e-18
SQRT2 = 2.0 ** 0.5

STEP = [
    ("sign_logit", 7, 0),
    ("x_quantize", 3, -1),
    ("x_turn", 2, -1),
    ("encode", 3, 0),
    ("logits", 6, 0),
    ("squash", 3, 0),
    ("encode", 3, 1),
    ("w_interleave", 2, 0),
    ("join", 1, -1),
    ("load_tile", 0, -1),
    ("h_quantize", 5, -1),
    ("w_interleave", 2, 1),
    ("h_gain", 4, 0),
    ("total", 68, -1),
    ("mask", 0, -1),
    ("recons", 33, 0),
    ("load_w_for", 1, -1),
    ("sign_logit", 7, 1),
    ("unmask", 0, -1),
    ("gain", 2, -1),
    ("squash", 3, 1),
    ("w_widen", 1, 0),
    ("h_turn", 3, 0),
    ("pick_bar", 0, -1),
    ("diff", 34, 0),
    ("logarithm", 29, -1),
    ("smaller", 40, -1),
    ("diff", 35, 1),
    ("h_gain", 4, 1),
    ("w_interleave", 2, 2),
    ("pick_x", 0, -1),
    ("square", 50, -1),
    ("recons", 34, 1),
    ("load_we", 2, -1),
    ("w_quantize", 3, -1),
    ("logits", 6, 1),
    ("w_interleave", 2, 3),
    ("w_drain", 2, 0),
    ("w_widen", 1, 1),
    ("w_drain", 2, 1),
    ("h_turn", 3, 1),
    ("sigm", 13, -1),
]
STEPS = 76

FLOPS = 3 * 2 * N * D * F


def tile_vimemaskandfeaturepretextloss_w4_kernel(
    tc, x, xbar, u, s, we_words, we_scales, g, wh_bytes, wh_scale, out
):
    nc = tc.nc
    with ExitStack() as ctx:
        keep = ctx.enter_context(tc.tile_pool(name="keep", bufs=1))
        pool = ctx.enter_context(tc.tile_pool(name="pool", bufs=2))
        psum = ctx.enter_context(tc.psum_pool(name="psum", bufs=1))
        ctx.enter_context(tc.manual_schedule())

        x_sb, u_sb, xb_sb, m_sb, x_ps, xg_sb, x8, xs8 = {}, {}, {}, {}, {}, {}, {}, {}
        z_ps, th_sb, ht_ps, hg_sb, h8, hs8 = {}, {}, {}, {}, {}, {}
        wb_sb, wide_sb, w_ps, wi_sb = {}, {}, {}, {}
        a_ps, r_ps, y_sb, l_sb, d_sb = {}, {}, {}, {}, {}

        def rows(i):
            return slice(i * P, (i + 1) * P)

        def load_tile(i):
            u_sb[i] = pool.tile([P, D], BF16, tag="u", name="u_t", bufs=4)
            nc.sync.dma_start(out=u_sb[i][:], in_=u[rows(i), :])
            xb_sb[i] = pool.tile([P, D], BF16, tag="xb", name="xb_t", bufs=4)
            nc.sync.dma_start(out=xb_sb[i][:], in_=xbar[rows(i), :])
            x_sb[i] = keep.tile([P, D], BF16, tag="x%d" % i, name="x_t")
            nc.sync.dma_start(out=x_sb[i][:], in_=x[rows(i), :])

        def load_w(j, gg):
            wb_sb[j, gg] = pool.tile([P, 4, D], U8, tag="wb", name="wb_t", bufs=2, align_bytes=64)
            nc.sync.dma_start(
                out=wb_sb[j, gg][:],
                in_=wh_bytes[j].rearrange("(g p t) n -> g p t n", p=P, t=4)[gg],
            )

        one = keep.tile([P, 1], BF16, tag="one", name="one")
        nc.vector.memset(one[:], 1.0)
        wes = keep.tile([P, 2, F], U8, tag="wes", name="wes", align_bytes=64)
        nc.vector.memset(wes[:].rearrange("p g n -> p (g n)").bitcast(U32), 0)
        dummy = keep.tile([P, 1], F32, tag="dummy", name="dummy")
        nc.scalar.activation(out=dummy[:], in_=one[:], func=ACT.Sigmoid)

        wsc = keep.tile([P, 2, 4], F32, tag="wsc", name="wsc")
        gcol = keep.tile([P, 2, 4], BF16, tag="gcol", name="gcol")
        scol = keep.tile([P, 2, 4], BF16, tag="scol", name="scol")
        nc.scalar.dma_start(out=scol[:], in_=s.rearrange("(g p t) -> p g t", p=P, t=4))
        nc.scalar.dma_start(out=wsc[:], in_=wh_scale.rearrange("o (g p t) e -> p g (t o e)", p=P, t=4))
        nc.scalar.dma_start(out=gcol[:], in_=g.rearrange("(c p t) -> p c t", p=P, t=4))

        we = keep.tile([P, 2, 2 * F], U8, tag="we", name="we", align_bytes=64)

        def load_we(i):
            nc.sync.dma_start(out=we[:], in_=we_words.rearrange("g p b -> p g b"))
            for q in range(4):
                nc.sync.dma_start(
                    out=wes[32 * q : 32 * q + 4, :, :].bitcast(I32),
                    in_=we_scales[:, 4 * q : 4 * q + 4, :].bitcast(I32).rearrange("g q n -> q g n"),
                )

        def load_w_for(k):
            if k in (0, 1, 4, 5):
                load_w(k // 4, k % 2)

        ident = keep.tile([P, P], F32, tag="ident", name="ident")
        make_identity(nc, ident[:])
        ident_b = keep.tile([P, P], BF16, tag="ident_b", name="ident_b")
        nc.vector.tensor_copy(out=ident_b[:], in_=ident[:])

        w8 = {}
        ws8 = {}
        for j in range(2):
            w8[j] = keep.tile([P, 2, D], U32, tag="w8_%d" % j, name="w8_t", align_bytes=64)
            ws8[j] = keep.tile([P, 2, D], U8, tag="ws8_%d" % j, name="ws8_t", align_bytes=64)

        def w_key(k):
            return k // 4, k % 2, (k // 2) % 2

        def w_widen(k, th):
            j, gg, nh = w_key(k)
            if th == 0:
                wide_sb[k] = pool.tile([P, 4, 512], BF16, tag="wide", name="wide_t", bufs=3)
            for t in (2 * th, 2 * th + 1):
                nc.scalar.activation(
                    out=wide_sb[k][:, t, :],
                    in_=wb_sb[j, gg][:, t, 512 * nh : 512 * (nh + 1)].bitcast(FP8),
                    func=ACT.Copy,
                    scale=wsc[:, gg, t : t + 1],
                )

        def w_interleave(k, part):
            b, q = part // 2, part % 2
            if q == 0:
                w_ps[k, b] = psum.tile([P, 1024], BF16, tag="p", name="w_ps_t", bufs=4)
            nc.tensor.matmul(
                out=w_ps[k, b][:, 512 * q : 512 * (q + 1)].rearrange("p (n t) -> p n t", t=4),
                lhsT=ident_b[:],
                rhs=wide_sb[k][:, :, P * part : P * (part + 1)].rearrange("p t n -> p n t"),
                start=True,
                stop=True,
            )

        def w_drain(k, b):
            if b == 0:
                wi_sb[k] = pool.tile([P, 2048], BF16, tag="wi", name="wi_t", bufs=2, align_bytes=64)
            nc.scalar.copy(out=wi_sb[k][:, 1024 * b : 1024 * (b + 1)], in_=w_ps[k, b][:])

        def w_quantize(k):
            j, gg, nh = w_key(k)
            cols = slice(512 * nh, 512 * (nh + 1))
            nc.vector.quantize_mx(
                out=w8[j][:, gg, cols].bitcast(FP8X4), scales=ws8[j][:, gg, cols], in_=wi_sb[k][:]
            )

        def mask(i):
            m_sb[i] = keep.tile([P, D], BF16, tag="m%d" % i, name="m_t")
            nc.vector.tensor_scalar(out=m_sb[i][:], in0=u_sb[i][:], scalar1=P_HIT, scalar2=None, op0=ALU.is_lt)

        def unmask(i):
            nc.vector.tensor_scalar(out=u_sb[i][:], in0=u_sb[i][:], scalar1=P_HIT, scalar2=None, op0=ALU.is_ge)

        def pick_bar(i):
            nc.vector.tensor_tensor(out=xb_sb[i][:], in0=m_sb[i][:], in1=xb_sb[i][:], op=ALU.mult)

        def pick_x(i):
            nc.vector.tensor_tensor(out=u_sb[i][:], in0=u_sb[i][:], in1=x_sb[i][:], op=ALU.mult)

        def join(i):
            nc.vector.tensor_tensor(out=xb_sb[i][:], in0=xb_sb[i][:], in1=u_sb[i][:], op=ALU.add)

        def x_turn(i):
            x_ps[i] = psum.tile([P, 4, P], F32, tag="p", name="x_ps_t", bufs=4)
            words = xb_sb[i][:].bitcast(F32)
            for gg in range(2):
                for v in range(2):
                    nc.tensor.transpose(
                        x_ps[i][:, 2 * gg + v, :], words[:, 256 * gg + v : 256 * (gg + 1) : 2], ident[:]
                    )

        def gain(i):
            xg_sb[i] = pool.tile([P, D], BF16, tag="xg", name="xg_t", bufs=2, align_bytes=64)
            for gg in range(2):
                nc.vector.tensor_tensor(
                    out=xg_sb[i][:, 512 * gg : 512 * (gg + 1)].rearrange("p (r v e) -> p r v e", v=2, e=2),
                    in0=x_ps[i][:, 2 * gg : 2 * gg + 2, :]
                    .rearrange("p v r -> p (v r)")
                    .bitcast(BF16)
                    .rearrange("p (v r e) -> p r v e", v=2, e=2),
                    in1=scol[:, gg, :].rearrange("p (v e) -> p v e", e=2).unsqueeze(1).to_broadcast([P, P, 2, 2]),
                    op=ALU.mult,
                )

        def x_quantize(i):
            x8[i] = pool.tile([P, 256], U32, tag="x8", name="x8_t", bufs=2, align_bytes=64)
            xs8[i] = pool.tile([P, 256], U8, tag="xs8", name="xs8_t", bufs=2, align_bytes=64)
            nc.vector.quantize_mx(out=x8[i][:].bitcast(FP8X4), scales=xs8[i][:], in_=xg_sb[i][:])

        def encode(i, c):
            z_ps[i, c] = psum.tile([P, 512], F32, tag="z", name="z_ps_t", bufs=2)
            for gg in range(2):
                nc.tensor.matmul_mx(
                    out=z_ps[i, c][:],
                    lhsT=x8[i][:, P * gg : P * (gg + 1)].bitcast(FP8X4),
                    lhsT_scale=xs8[i][:, P * gg : P * (gg + 1)],
                    rhs=we[:, gg, 1024 * c : 1024 * (c + 1)].bitcast(FP4X4),
                    rhs_scale=wes[:, gg, 512 * c : 512 * (c + 1)],
                    start=(gg == 0),
                    stop=(gg == 1),
                )

        def squash(i, c):
            th_sb[i, c] = pool.tile([P, 4, P], F32, tag="th", name="th_t", bufs=3)
            nc.scalar.activation(
                out=th_sb[i, c][:], in_=z_ps[i, c][:].rearrange("p (m t) -> p t m", t=4), func=ACT.Tanh
            )

        def h_turn(i, c):
            ht_ps[i, c] = psum.tile([P, 4, P], F32, tag="h", name="ht_ps_t", bufs=2)
            for t in range(4):
                nc.tensor.transpose(ht_ps[i, c][:, t, :], th_sb[i, c][:, t, :], ident[:])

        def h_gain(i, c):
            if c == 0:
                hg_sb[i] = pool.tile([P, F], BF16, tag="hg", name="hg_t", bufs=2, align_bytes=64)
            nc.vector.tensor_tensor(
                out=hg_sb[i][:, 512 * c : 512 * (c + 1)].rearrange("p (r t) -> p r t", t=4),
                in0=ht_ps[i, c][:].rearrange("p t r -> p r t"),
                in1=gcol[:, c, :].unsqueeze(1).to_broadcast([P, P, 4]),
                op=ALU.mult,
            )

        def h_quantize(i):
            h8[i] = keep.tile([P, 256], U32, tag="h8_%d" % i, name="h8_t", align_bytes=64)
            hs8[i] = keep.tile([P, 256], U8, tag="hs8_%d" % i, name="hs8_t", align_bytes=64)
            nc.vector.quantize_mx(out=h8[i][:].bitcast(FP8X4), scales=hs8[i][:], in_=hg_sb[i][:])

        def head(i, j, nh, tag):
            bank = psum.tile([P, 512], F32, tag=tag, name="head_ps_t", bufs=4 if tag == "p" else 2)
            cols = slice(512 * nh, 512 * (nh + 1))
            for gg in range(2):
                nc.tensor.matmul_mx(
                    out=bank[:],
                    lhsT=h8[i][:, P * gg : P * (gg + 1)].bitcast(FP8X4),
                    lhsT_scale=hs8[i][:, P * gg : P * (gg + 1)],
                    rhs=w8[j][:, gg, cols].bitcast(FP8X4),
                    rhs_scale=ws8[j][:, gg, cols],
                    start=(gg == 0),
                    stop=(gg == 1),
                )
            return bank

        def logits(i, nh):
            a_ps[i, nh] = head(i, 0, nh, "p")

        def recons(i, nh):
            r_ps[i, nh] = head(i, 1, nh, "zp"[nh])

        def sign_logit(i, nh):
            if nh == 0:
                y_sb[i] = keep.tile([P, D], F32, tag="y%d" % i, name="y_t")
            cols = slice(512 * nh, 512 * (nh + 1))
            nc.vector.scalar_tensor_tensor(
                out=y_sb[i][:, cols], in0=m_sb[i][:, cols], scalar=0.5, in1=a_ps[i, nh][:],
                op0=ALU.subtract, op1=ALU.mult,
            )

        def sigm(i):
            l_sb[i] = keep.tile([P, D], F32, tag="l%d" % i, name="l_t")
            nc.scalar.activation(out=l_sb[i][:], in_=y_sb[i][:], func=ACT.Sigmoid, scale=2.0)

        def diff(i, nh):
            if nh == 0:
                d_sb[i] = keep.tile([P, D], F32, tag="d%d" % i, name="d_t")
            cols = slice(512 * nh, 512 * (nh + 1))
            nc.vector.tensor_tensor(
                out=d_sb[i][:, cols], in0=r_ps[i, nh][:], in1=x_sb[i][:, cols], op=ALU.subtract
            )

        def square(i):
            nc.scalar.activation(out=d_sb[i][:], in_=d_sb[i][:], func=ACT.Square, scale=SQRT2)

        def logarithm(i):
            nc.scalar.activation(out=l_sb[i][:], in_=l_sb[i][:], func=ACT.Ln, bias=LN_FLOOR)

        def smaller(i):
            nc.vector.scalar_tensor_tensor(
                out=y_sb[i][:], in0=y_sb[i][:], scalar=2.0, in1=l_sb[i][:], op0=ALU.mult, op1=ALU.min
            )

        def total(i):
            parts = 2 if i == T - 1 else 1
            for part in range(parts):
                cols = slice(part * D // parts, (part + 1) * D // parts)
                nc.vector.tensor_tensor(
                    out=d_sb[i][:, cols], in0=d_sb[i][:, cols], in1=y_sb[i][:, cols], op=ALU.subtract
                )
                nc.sync.dma_start(out=out[rows(i), cols], in_=d_sb[i][:, cols])

        calls = dict(
            load_tile=load_tile, load_we=load_we, load_w_for=load_w_for, mask=mask, unmask=unmask,
            pick_bar=pick_bar, pick_x=pick_x, join=join, gain=gain, x_turn=x_turn,
            x_quantize=x_quantize, encode=encode, squash=squash, h_turn=h_turn, h_gain=h_gain,
            h_quantize=h_quantize, w_widen=w_widen, w_interleave=w_interleave, w_drain=w_drain,
            w_quantize=w_quantize, logits=logits, sign_logit=sign_logit, sigm=sigm, recons=recons,
            diff=diff, square=square, logarithm=logarithm, smaller=smaller, total=total,
        )
        for step in range(STEPS):
            for what, lag, half in STEP:
                i = step - lag
                if 0 <= i < (1 if what == "load_we" else T):
                    if half < 0:
                        calls[what](i)
                    else:
                        calls[what](i, half)
